import numpy as np
import ml_dtypes


def mxq(x, axis, fmt="e4m3"):
    dtype, down = {"e4m3": (ml_dtypes.float8_e4m3fn, 7), "e5m2": (ml_dtypes.float8_e5m2, 14)}[fmt]
    v = np.moveaxis(np.asarray(x, np.float32).astype(ml_dtypes.bfloat16).astype(np.float64), axis, -1)
    blocks = v.reshape(v.shape[:-1] + (-1, 32))
    amax = np.abs(blocks).max(-1, keepdims=True)
    byte = np.maximum(np.where(amax > 0, np.frexp(amax)[1] - 1 + 127, 0) - down, 1)
    scale = np.exp2(byte - 127.0)
    codes = (blocks / scale).astype(np.float32).astype(dtype).astype(np.float64)
    return np.moveaxis((codes * scale).reshape(v.shape), -1, axis)


WIDE = False


def mx_kscale(k):
    if not WIDE:
        return np.ones(k)
    levels = np.array([10, -10, 5, -5, 0])
    if k % 512:
        return np.exp2(np.random.permutation(np.resize(levels, k // 32))).repeat(32)
    a = np.empty((k // 512, 16))
    for p in range(k // 512):
        a[p, :8] = np.random.permutation(np.resize(levels, 8))
        for g in range(8):
            far = levels[np.abs(levels - a[p, g]) >= 10]
            a[p, g + 8] = far[np.random.randint(len(far))]
    return np.exp2(a.ravel()).repeat(32)


def f64(x):
    return np.asarray(x).astype(np.float64)


def striped(idx):
    return np.tile(idx.reshape(-1, 16).T, (8, 1)).astype(np.uint16)


def unstriped(offs):
    return offs[:16].T.reshape(-1).astype(np.int64)


def striped8(idx):
    return np.concatenate([v.reshape(-1, 16).T for v in idx]).astype(np.uint16)


def unstriped8(offs):
    return np.stack([offs[16 * g:16 * g + 16].T.reshape(-1) for g in range(8)]).astype(np.int64)


E2M1 = np.array([0.0, 0.5, 1.0, 1.5, 2.0, 3.0, 4.0, 6.0, -0.0, -0.5, -1.0, -1.5, -2.0, -3.0, -4.0, -6.0])


def pack_weight(w, fmt):
    k, n = w.shape
    w = f64(np.asarray(w, np.float32).astype(ml_dtypes.bfloat16)).reshape(k // 32, 32, n)
    amax = np.abs(w).max(1)
    if fmt == "e4m3":
        byte = np.frexp(amax)[1] - 1 + 127 - 7
    else:
        mant, ex = np.frexp(amax / 6.0)
        byte = np.where(mant > 0.5, ex, ex - 1) + 127
    byte = np.clip(np.where(amax > 0, byte, 1), 1, 254)
    scaled = (w * np.exp2(127.0 - byte)[:, None, :]).reshape(k, n).astype(np.float32)
    by_word = np.ascontiguousarray(scaled.reshape(k // 512, 128, 4, n).transpose(0, 1, 3, 2))
    if fmt == "e4m3":
        words = by_word.astype(ml_dtypes.float8_e4m3fn).view(np.uint8)
    else:
        c = by_word.astype(ml_dtypes.float4_e2m1fn).view(np.uint8) & 0xF
        words = (c[..., 0::2] | (c[..., 1::2] << 4)).reshape(k // 512, 128, 2 * n)
    return np.ascontiguousarray(words), np.ascontiguousarray(byte.astype(np.uint8).reshape(k // 512, 16, n))


def unpack_weight(words, scales, fmt):
    g, _, n = scales.shape
    words = np.ascontiguousarray(words).reshape(g, 128, n, -1)
    if fmt == "e4m3":
        vals = words.view(ml_dtypes.float8_e4m3fn).astype(np.float64)
    else:
        nib = np.empty((g, 128, n, 4), np.uint8)
        nib[..., 0::2] = words & 0xF
        nib[..., 1::2] = words >> 4
        vals = E2M1[nib]
    vals = vals * np.repeat(np.exp2(scales.astype(np.float64) - 127.0), 8, axis=1)[..., None]
    return vals.transpose(0, 1, 3, 2).reshape(g * 512, n)


def pack_table(v):
    words, scales = pack_weight(v, "e4m3")
    return np.concatenate([words.reshape(words.shape[0], -1), scales.reshape(scales.shape[0], -1)], axis=1)


def unpack_table(tab):
    g, t = tab.shape[0], tab.shape[1] // 528
    return unpack_weight(tab[:, :512 * t].reshape(g, 128, t, 4), tab[:, 512 * t:].reshape(g, 16, t), "e4m3")


def silu(v):
    return v / (1.0 + np.exp(-np.maximum(v, -700.0)))


K, M, T, S = 2048, 1024, 512, 256


def setup_inputs():
    n = np.random.standard_normal
    s = mx_kscale(K)[:, None]
    w = n((K, M)) / np.sqrt(K) / s
    p_w4 = pack_weight(w[512:], "e2m1")
    return {
        "tab": pack_table(n((K, T)) * s),
        "w8": (w[:512]).astype(np.float32),
        "w4_words": p_w4[0],
        "w4_scales": p_w4[1],
        "b": (0.3 * n(1024)).astype(np.float32),
        "wgo": np.repeat(np.random.uniform(0.5, 2.0, (8, S)), 16, axis=0).astype(np.float32),
        "offs": striped(np.random.permutation(T)[:S]),
        "offs2": striped8(np.stack([np.random.permutation(T)[:S] for _ in range(8)])),
    }


def reference(tab, w8, w4_words, w4_scales, b, wgo, offs, offs2):
    tab_ = unpack_table(tab)[:, unstriped(offs)]
    w8_ = mxq(f64(w8), 0, "e4m3")
    w4_ = unpack_weight(w4_words, w4_scales, "e2m1")
    y = w8_.T @ tab_[:512] + w4_.T @ tab_[512:]
    place = unstriped8(offs2)[np.arange(M) % 128 // 16]
    out = np.zeros((M, T))
    out[np.arange(M)[:, None], place] = f64(wgo)[np.arange(M) % 128] * (silu(y + f64(b)[:, None]))
    return out

@@ -1,0 +1,180 @@
+from contextlib import ExitStack
+
+import concourse.mybir as mybir
+from concourse.masks import make_identity
+
+K, M, T, S = 2048, 1024, 512, 256
+FLOPS = 2 * K * M * S
+
+F32 = mybir.dt.float32
+BF16 = mybir.dt.bfloat16
+I32 = mybir.dt.int32
+U32 = mybir.dt.uint32
+U16 = mybir.dt.uint16
+U8 = mybir.dt.uint8
+FP8X4 = mybir.dt.float8_e4m3fn_x4
+FP4X4 = mybir.dt.float4_e2m1fn_x4
+SILU = mybir.ActivationFunctionType.Silu
+MULT = mybir.AluOpType.mult
+
+P = 128
+PACK = 4
+PASSES = K // (P * PACK)
+ROW_TILES = M // P
+HALF = S // 2
+WORD_BYTES = P * PACK * T
+W8_CHUNKS = (128, 128, 128, 128, 256, 256)
+W4_CHUNKS = (256, 256, 512)
+PAGES = 4
+
+
+def tile_list_tabhs_o_silu_kernel(tc, tab, w8, w4_words, w4_scales, b, wgo, offs, offs2, out):
+    nc = tc.nc
+    with ExitStack() as ctx:
+        held = ctx.enter_context(tc.tile_pool(name="held", bufs=1))
+        psum = ctx.enter_context(tc.psum_pool(name="psum", bufs=1))
+
+        pick = held.tile([P, S // 16], U16, name="pick")
+        place = held.tile([P, S // 16], U16, name="place")
+        tab_scales = held.tile([P, PASSES, T], U8, name="tab_scales", tag="scale_window", align_bytes=64)
+        w4_planes = held.tile([P, PASSES - 1, M], U8, name="w4_planes", align_bytes=64)
+        b_rows = held.tile([P, P], F32, name="b_rows")
+        warm_in = held.tile([P, 1], F32, name="warm_in")
+        warm_out = held.tile([P, 1], F32, name="warm_out")
+        identity = held.tile([P, P], F32, name="identity")
+        pages = [held.tile([P, T], F32, name=f"page{i}") for i in range(2)]
+
+        nc.vector.memset(tab_scales[:].bitcast(I32), 0)
+        nc.vector.memset(warm_in[:], 0.0)
+        nc.vector.memset(w4_planes[:].bitcast(I32), 0)
+        nc.gpsimd.memset(b_rows[:], 0.0)
+        nc.gpsimd.dma_start(b_rows[0:ROW_TILES, :], b.rearrange("(i p) -> i p", p=P))
+        make_identity(nc, identity[:])
+        for page in pages:
+            nc.vector.memset(page[:], 0.0)
+
+        nc.sync.dma_start(pick[:], offs)
+        nc.scalar.activation(out=warm_out[:], in_=warm_in[:], func=SILU)
+
+        w8_rows = w8.rearrange("(p i) n -> p i n", i=PACK)
+        w8_starts = [sum(W8_CHUNKS[:c]) for c in range(len(W8_CHUNKS))]
+        w8_raw = [held.tile([P, PACK, w], F32, name=f"w8_raw{c}", tag=f"raw{c}") for c, w in enumerate(W8_CHUNKS)]
+        w4_rows = w4_words.rearrange("a p x -> p a x")
+        w4_starts = [sum(W4_CHUNKS[:c]) for c in range(len(W4_CHUNKS))]
+        w4_codes = [held.tile([P, PASSES - 1, 2 * w], U8, name=f"w4_codes{c}", align_bytes=64) for c, w in enumerate(W4_CHUNKS)]
+
+        def load_w8(c):
+            nc.sync.dma_start(w8_raw[c][:], w8_rows[:, :, w8_starts[c] : w8_starts[c] + W8_CHUNKS[c]])
+
+        def load_w4(c):
+            cols = slice(2 * w4_starts[c], 2 * (w4_starts[c] + W4_CHUNKS[c]))
+            nc.sync.dma_start(w4_codes[c][:].bitcast(I32), w4_rows[:, :, cols].bitcast(I32))
+
+        tab_word_rows = tab[:, :WORD_BYTES].rearrange("a (p x) -> p a x", p=P).bitcast(I32)
+        tab_words = [held.tile([P, 2, T], I32, name=f"tab_words{h}", tag=f"shared{h}") for h in range(2)]
+        nc.sync.dma_start(tab_words[0][:], tab_word_rows[:, 0:2, :])
+        tab_scale_rows = tab[:, WORD_BYTES:].rearrange("a (q t) -> q a t", t=T).bitcast(I32)
+        for quad in range(4):
+            nc.sync.dma_start(tab_scales[32 * quad : 32 * quad + 4].bitcast(I32), tab_scale_rows[4 * quad : 4 * quad + 4])
+        load_w8(0)
+        nc.sync.dma_start(tab_words[1][:], tab_word_rows[:, 2:4, :])
+        load_w4(0)
+        w4_scale_rows = w4_scales.rearrange("a q n -> q a n").bitcast(I32)
+        for quad in range(4):
+            nc.sync.dma_start(w4_planes[32 * quad : 32 * quad + 4].bitcast(I32), w4_scale_rows[4 * quad : 4 * quad + 4])
+        nc.sync.dma_start(place[:], offs2)
+        gain = held.tile([P, S], F32, name="gain")
+        nc.sync.dma_start(gain[:], wgo)
+        load_w8(1)
+        load_w8(2)
+        load_w8(3)
+        load_w4(1)
+        load_w8(4)
+        load_w4(2)
+        load_w8(5)
+
+        w8_codes = [held.tile([P, w], U32, name=f"w8_codes{c}", align_bytes=64) for c, w in enumerate(W8_CHUNKS)]
+        w8_planes = [held.tile([P, w], U8, name=f"w8_planes{c}", align_bytes=64) for c, w in enumerate(W8_CHUNKS)]
+
+        def chunk_of(starts, n0):
+            c = max(j for j, s in enumerate(starts) if s <= n0)
+            return c, n0 - starts[c]
+
+        def quantise_w8(c):
+            grouped = held.tile([P, W8_CHUNKS[c], PACK], BF16, name=f"w8_grouped{c}", tag=f"staged{c}", align_bytes=64)
+            for o in range(0, W8_CHUNKS[c], P):
+                nc.scalar.copy(
+                    out=grouped[:, o : o + P, :].rearrange("p (c j) i -> p c i j", j=4),
+                    in_=w8_raw[c][:, :, o : o + P].rearrange("p i (c j) -> p c i j", j=4),
+                )
+            nc.vector.quantize_mx(
+                out=w8_codes[c][:].bitcast(FP8X4),
+                scales=w8_planes[c][:],
+                in_=grouped[:].rearrange("p n i -> p (n i)"),
+            )
+
+        v_codes, v_scales = [], []
+
+        def gather_words(h, tag):
+            pair = held.tile([P, 2, S], U32, name=f"v_codes{h}", tag=tag, align_bytes=64)
+            for j in range(2):
+                nc.vector.tensor_copy(pair[:, j, :], tab_words[h][:, j, :].bitcast(U32).indirect(pick[:]))
+                v_codes.append(pair[:, j, :])
+
+        gather_words(0, "v_codes0")
+        for a in range(PASSES):
+            if a == PASSES - 1:
+                quantise_w8(0)
+            tag = "staged0" if a == PASSES - 1 else f"v_scales{a}"
+            v_scales.append(held.tile([P, S], U8, name=f"v_scales{a}", tag=tag, align_bytes=64))
+            nc.vector.tensor_copy(v_scales[a][:], tab_scales[:, a, :].indirect(pick[:]))
+        gather_words(1, "scale_window")
+
+        b_turned = psum.tile([P, P], F32, name="b_turned", tag=f"bank{ROW_TILES - 1}")
+        nc.tensor.transpose(b_turned[:], b_rows[:], identity[:])
+        bias = held.tile([P, ROW_TILES], F32, name="bias")
+        nc.scalar.copy(out=bias[:], in_=b_turned[:, 0:ROW_TILES])
+
+        quantise_w8(1)
+        for h in range(2):
+            page = held.tile([P, T], F32, name=f"page{2 + h}", tag=f"shared{h}")
+            nc.vector.memset(page[:], 0.0)
+            pages.append(page)
+
+        for i in range(ROW_TILES):
+            n0 = i * P
+            c8, o8 = chunk_of(w8_starts, n0)
+            last_of_chunk = o8 + P == W8_CHUNKS[c8]
+            if last_of_chunk and 0 < c8 < len(W8_CHUNKS) - 1:
+                quantise_w8(c8 + 1)
+            c4, o4 = chunk_of(w4_starts, n0)
+            y = psum.tile([P, S], F32, name=f"y{i}", tag=f"bank{i}")
+            steps = [(a, h) for a in range(1, PASSES) for h in range(2)]
+            steps = [(0, 0)] + steps if i == 0 else steps + [(0, 0)]
+            for j, (a, h) in enumerate(steps):
+                flags = dict(start=(j == 0), stop=(j == len(steps) - 1))
+                if a == 0:
+                    nc.tensor.matmul_mx(
+                        out=y[:],
+                        lhsT=w8_codes[c8][:, o8 : o8 + P].bitcast(FP8X4),
+                        lhsT_scale=w8_planes[c8][:, o8 : o8 + P],
+                        rhs=v_codes[0].bitcast(FP8X4),
+                        rhs_scale=v_scales[0][:],
+                        **flags,
+                    )
+                else:
+                    cols = slice(h * HALF, (h + 1) * HALF)
+                    nc.tensor.matmul_mx(
+                        out=y[:, cols],
+                        lhsT=w4_codes[c4][:, a - 1, 2 * o4 : 2 * (o4 + P)].bitcast(FP4X4),
+                        lhsT_scale=w4_planes[:, a - 1, n0 : n0 + P],
+                        rhs=v_codes[a][:, cols].bitcast(FP8X4),
+                        rhs_scale=v_scales[a][:, cols],
+                        **flags,
+                    )
+            tag = f"raw{c8 + 1}" if last_of_chunk else f"act{i}"
+            act = held.tile([P, S], F32, name=f"act{i}", tag=tag)
+            nc.scalar.activation(out=act[:], in_=y[:], func=SILU, bias=bias[:, i : i + 1])
+            page = pages[i % PAGES]
+            nc.vector.tensor_tensor(page[:].indirect(place[:]), act[:], gain[:], MULT)
+            nc.sync.dma_start(out[n0 : n0 + P, :], page[:])

@@ -42,7 +42,7 @@ def tile_list_tabhs_o_silu_kernel(tc, tab, w8, w4_words, w4_scales, b, wgo, offs
         warm_in = held.tile([P, 1], F32, name="warm_in")
         warm_out = held.tile([P, 1], F32, name="warm_out")
         identity = held.tile([P, P], F32, name="identity")
-        pages = [held.tile([P, T], F32, name=f"page{i}") for i in range(2)]
+        pages = [held.tile([P, T], F32, name=f"page{i}") for i in range(PAGES)]
 
         nc.vector.memset(tab_scales[:].bitcast(I32), 0)
         nc.vector.memset(warm_in[:], 0.0)
@@ -50,8 +50,10 @@ def tile_list_tabhs_o_silu_kernel(tc, tab, w8, w4_words, w4_scales, b, wgo, offs
         nc.gpsimd.memset(b_rows[:], 0.0)
         nc.gpsimd.dma_start(b_rows[0:ROW_TILES, :], b.rearrange("(i p) -> i p", p=P))
         make_identity(nc, identity[:])
-        for page in pages:
-            nc.vector.memset(page[:], 0.0)
+        gain = held.tile([P, S], F32, name="gain")
+        nc.gpsimd.dma_start(gain[:], wgo)
+        for i, page in enumerate(pages):
+            (nc.vector if i < 2 else nc.gpsimd).memset(page[:], 0.0)
 
         nc.sync.dma_start(pick[:], offs)
         nc.scalar.activation(out=warm_out[:], in_=warm_in[:], func=SILU)
@@ -71,21 +73,20 @@ def tile_list_tabhs_o_silu_kernel(tc, tab, w8, w4_words, w4_scales, b, wgo, offs
             nc.sync.dma_start(w4_codes[c][:].bitcast(I32), w4_rows[:, :, cols].bitcast(I32))
 
         tab_word_rows = tab[:, :WORD_BYTES].rearrange("a (p x) -> p a x", p=P).bitcast(I32)
-        tab_words = [held.tile([P, 2, T], I32, name=f"tab_words{h}", tag=f"shared{h}") for h in range(2)]
-        nc.sync.dma_start(tab_words[0][:], tab_word_rows[:, 0:2, :])
+        groups = ((0, 1), (1, PASSES))
+        tab_words = [held.tile([P, a1 - a0, T], I32, name=f"tab_words{a0}") for a0, a1 in groups]
+        nc.sync.dma_start(tab_words[0][:], tab_word_rows[:, 0:1, :])
         tab_scale_rows = tab[:, WORD_BYTES:].rearrange("a (q t) -> q a t", t=T).bitcast(I32)
         for quad in range(4):
             nc.sync.dma_start(tab_scales[32 * quad : 32 * quad + 4].bitcast(I32), tab_scale_rows[4 * quad : 4 * quad + 4])
         load_w8(0)
-        nc.sync.dma_start(tab_words[1][:], tab_word_rows[:, 2:4, :])
+        nc.sync.dma_start(tab_words[1][:], tab_word_rows[:, 1:PASSES, :])
         load_w4(0)
         w4_scale_rows = w4_scales.rearrange("a q n -> q a n").bitcast(I32)
         for quad in range(4):
             nc.sync.dma_start(w4_planes[32 * quad : 32 * quad + 4].bitcast(I32), w4_scale_rows[4 * quad : 4 * quad + 4])
-        nc.sync.dma_start(place[:], offs2)
-        gain = held.tile([P, S], F32, name="gain")
-        nc.sync.dma_start(gain[:], wgo)
         load_w8(1)
+        nc.sync.dma_start(place[:], offs2)
         load_w8(2)
         load_w8(3)
         load_w4(1)
@@ -115,20 +116,23 @@ def tile_list_tabhs_o_silu_kernel(tc, tab, w8, w4_words, w4_scales, b, wgo, offs
 
         v_codes, v_scales = [], []
 
-        def gather_words(h, tag):
-            pair = held.tile([P, 2, S], U32, name=f"v_codes{h}", tag=tag, align_bytes=64)
-            for j in range(2):
-                nc.vector.tensor_copy(pair[:, j, :], tab_words[h][:, j, :].bitcast(U32).indirect(pick[:]))
-                v_codes.append(pair[:, j, :])
-
-        gather_words(0, "v_codes0")
+        halves = [slice(h * HALF, (h + 1) * HALF) for h in range(2)]
+        list_halves = [slice(h * HALF // 16, (h + 1) * HALF // 16) for h in range(2)]
+        v_codes.append(held.tile([P, S], U32, name="v_codes0", align_bytes=64)[:])
+        nc.vector.tensor_copy(v_codes[0], tab_words[0][:, 0, :].bitcast(U32).indirect(pick[:]))
         for a in range(PASSES):
             if a == PASSES - 1:
                 quantise_w8(0)
             tag = "staged0" if a == PASSES - 1 else f"v_scales{a}"
             v_scales.append(held.tile([P, S], U8, name=f"v_scales{a}", tag=tag, align_bytes=64))
             nc.vector.tensor_copy(v_scales[a][:], tab_scales[:, a, :].indirect(pick[:]))
-        gather_words(1, "scale_window")
+        later = held.tile([P, (PASSES - 1) * S], U32, name="v_codes_later", tag="scale_window", align_bytes=64)
+        for a in range(1, PASSES):
+            v_codes.append(later[:, (a - 1) * S : a * S])
+        for h in range(2):
+            for a in range(1, PASSES):
+                window = tab_words[1][:, a - 1, :].bitcast(U32)
+                nc.vector.tensor_copy(v_codes[a][:, halves[h]], window.indirect(pick[:, list_halves[h]]))
 
         b_turned = psum.tile([P, P], F32, name="b_turned", tag=f"bank{ROW_TILES - 1}")
         nc.tensor.transpose(b_turned[:], b_rows[:], identity[:])
@@ -136,10 +140,6 @@ def tile_list_tabhs_o_silu_kernel(tc, tab, w8, w4_words, w4_scales, b, wgo, offs
         nc.scalar.copy(out=bias[:], in_=b_turned[:, 0:ROW_TILES])
 
         quantise_w8(1)
-        for h in range(2):
-            page = held.tile([P, T], F32, name=f"page{2 + h}", tag=f"shared{h}")
-            nc.vector.memset(page[:], 0.0)
-            pages.append(page)
 
         for i in range(ROW_TILES):
             n0 = i * P
@@ -148,33 +148,45 @@ def tile_list_tabhs_o_silu_kernel(tc, tab, w8, w4_words, w4_scales, b, wgo, offs
             if last_of_chunk and 0 < c8 < len(W8_CHUNKS) - 1:
                 quantise_w8(c8 + 1)
             c4, o4 = chunk_of(w4_starts, n0)
-            y = psum.tile([P, S], F32, name=f"y{i}", tag=f"bank{i}")
-            steps = [(a, h) for a in range(1, PASSES) for h in range(2)]
-            steps = [(0, 0)] + steps if i == 0 else steps + [(0, 0)]
-            for j, (a, h) in enumerate(steps):
-                flags = dict(start=(j == 0), stop=(j == len(steps) - 1))
-                if a == 0:
-                    nc.tensor.matmul_mx(
-                        out=y[:],
-                        lhsT=w8_codes[c8][:, o8 : o8 + P].bitcast(FP8X4),
-                        lhsT_scale=w8_planes[c8][:, o8 : o8 + P],
-                        rhs=v_codes[0].bitcast(FP8X4),
-                        rhs_scale=v_scales[0][:],
-                        **flags,
-                    )
-                else:
-                    cols = slice(h * HALF, (h + 1) * HALF)
-                    nc.tensor.matmul_mx(
-                        out=y[:, cols],
-                        lhsT=w4_codes[c4][:, a - 1, 2 * o4 : 2 * (o4 + P)].bitcast(FP4X4),
-                        lhsT_scale=w4_planes[:, a - 1, n0 : n0 + P],
-                        rhs=v_codes[a][:, cols].bitcast(FP8X4),
-                        rhs_scale=v_scales[a][:, cols],
-                        **flags,
-                    )
-            tag = f"raw{c8 + 1}" if last_of_chunk else f"act{i}"
-            act = held.tile([P, S], F32, name=f"act{i}", tag=tag)
-            nc.scalar.activation(out=act[:], in_=y[:], func=SILU, bias=bias[:, i : i + 1])
             page = pages[i % PAGES]
-            nc.vector.tensor_tensor(page[:].indirect(place[:]), act[:], gain[:], MULT)
+
+            def pass_e4m3(y, cols, **flags):
+                nc.tensor.matmul_mx(
+                    out=y,
+                    lhsT=w8_codes[c8][:, o8 : o8 + P].bitcast(FP8X4),
+                    lhsT_scale=w8_planes[c8][:, o8 : o8 + P],
+                    rhs=v_codes[0][:, cols].bitcast(FP8X4),
+                    rhs_scale=v_scales[0][:, cols],
+                    **flags,
+                )
+
+            def pass_e2m1(y, a, cols, **flags):
+                nc.tensor.matmul_mx(
+                    out=y,
+                    lhsT=w4_codes[c4][:, a - 1, 2 * o4 : 2 * (o4 + P)].bitcast(FP4X4),
+                    lhsT_scale=w4_planes[:, a - 1, n0 : n0 + P],
+                    rhs=v_codes[a][:, cols].bitcast(FP8X4),
+                    rhs_scale=v_scales[a][:, cols],
+                    **flags,
+                )
+
+            tag = f"raw{c8 + 1}" if last_of_chunk else f"act{i}"
+            if i == 0:
+                for h in range(2):
+                    y = psum.tile([P, HALF], F32, name=f"y0{h}", tag=("bank0", f"bank{ROW_TILES - 2}")[h])
+                    pass_e4m3(y[:], halves[h], start=True, stop=False)
+                    for a in range(1, PASSES):
+                        pass_e2m1(y[:], a, halves[h], start=False, stop=(a == PASSES - 1))
+                    act = held.tile([P, HALF], F32, name=f"act0{h}", tag=("act0", tag)[h])
+                    nc.scalar.activation(out=act[:], in_=y[:], func=SILU, bias=bias[:, i : i + 1])
+                    nc.vector.tensor_tensor(page[:].indirect(place[:, list_halves[h]]), act[:], gain[:, halves[h]], MULT)
+            else:
+                y = psum.tile([P, S], F32, name=f"y{i}", tag=f"bank{i}")
+                for a in range(1, PASSES):
+                    for h in range(2):
+                        pass_e2m1(y[:, halves[h]], a, halves[h], start=(a == 1 and h == 0), stop=False)
+                pass_e4m3(y[:], slice(0, S), start=False, stop=True)
+                act = held.tile([P, S], F32, name=f"act{i}", tag=tag)
+                nc.scalar.activation(out=act[:], in_=y[:], func=SILU, bias=bias[:, i : i + 1])
+                nc.vector.tensor_tensor(page[:].indirect(place[:]), act[:], gain[:], MULT)
             nc.sync.dma_start(out[n0 : n0 + P, :], page[:])

@@ -25,6 +25,7 @@ HALF = S // 2
 WORD_BYTES = P * PACK * T
 W8_CHUNKS = (128, 128, 128, 128, 256, 256)
 W4_CHUNKS = (256, 256, 512)
+PLANE_CHUNKS = (256, 768)
 PAGES = 4
 
 
@@ -37,23 +38,24 @@ def tile_list_tabhs_o_silu_kernel(tc, tab, w8, w4_words, w4_scales, b, wgo, offs
         pick = held.tile([P, S // 16], U16, name="pick")
         place = held.tile([P, S // 16], U16, name="place")
         tab_scales = held.tile([P, PASSES, T], U8, name="tab_scales", tag="scale_window", align_bytes=64)
-        w4_planes = held.tile([P, PASSES - 1, M], U8, name="w4_planes", align_bytes=64)
+        w4_planes = [held.tile([P, PASSES - 1, w], U8, name=f"w4_planes{c}", align_bytes=64) for c, w in enumerate(PLANE_CHUNKS)]
         b_rows = held.tile([P, P], F32, name="b_rows")
         warm_in = held.tile([P, 1], F32, name="warm_in")
         warm_out = held.tile([P, 1], F32, name="warm_out")
         identity = held.tile([P, P], F32, name="identity")
-        pages = [held.tile([P, T], F32, name=f"page{i}") for i in range(PAGES)]
+        pages = [held.tile([P, T], F32, name=f"page{i}") for i in range(2)]
 
         nc.vector.memset(tab_scales[:].bitcast(I32), 0)
         nc.vector.memset(warm_in[:], 0.0)
-        nc.vector.memset(w4_planes[:].bitcast(I32), 0)
+        for planes in w4_planes:
+            nc.vector.memset(planes[:].bitcast(I32), 0)
         nc.gpsimd.memset(b_rows[:], 0.0)
         nc.gpsimd.dma_start(b_rows[0:ROW_TILES, :], b.rearrange("(i p) -> i p", p=P))
         make_identity(nc, identity[:])
         gain = held.tile([P, S], F32, name="gain")
         nc.gpsimd.dma_start(gain[:], wgo)
-        for i, page in enumerate(pages):
-            (nc.vector if i < 2 else nc.gpsimd).memset(page[:], 0.0)
+        for page in pages:
+            nc.vector.memset(page[:], 0.0)
 
         nc.sync.dma_start(pick[:], offs)
         nc.scalar.activation(out=warm_out[:], in_=warm_in[:], func=SILU)
@@ -74,7 +76,7 @@ def tile_list_tabhs_o_silu_kernel(tc, tab, w8, w4_words, w4_scales, b, wgo, offs
 
         tab_word_rows = tab[:, :WORD_BYTES].rearrange("a (p x) -> p a x", p=P).bitcast(I32)
         groups = ((0, 1), (1, PASSES))
-        tab_words = [held.tile([P, a1 - a0, T], I32, name=f"tab_words{a0}") for a0, a1 in groups]
+        tab_words = [held.tile([P, a1 - a0, T], I32, name=f"tab_words{a0}", tag=f"words{a0}", align_bytes=64) for a0, a1 in groups]
         nc.sync.dma_start(tab_words[0][:], tab_word_rows[:, 0:1, :])
         tab_scale_rows = tab[:, WORD_BYTES:].rearrange("a (q t) -> q a t", t=T).bitcast(I32)
         for quad in range(4):
@@ -82,12 +84,22 @@ def tile_list_tabhs_o_silu_kernel(tc, tab, w8, w4_words, w4_scales, b, wgo, offs
         load_w8(0)
         nc.sync.dma_start(tab_words[1][:], tab_word_rows[:, 1:PASSES, :])
         load_w4(0)
-        w4_scale_rows = w4_scales.rearrange("a q n -> q a n").bitcast(I32)
-        for quad in range(4):
-            nc.sync.dma_start(w4_planes[32 * quad : 32 * quad + 4].bitcast(I32), w4_scale_rows[4 * quad : 4 * quad + 4])
-        load_w8(1)
+        w4_scale_rows = w4_scales.rearrange("a q n -> q a n")
+        plane_starts = [sum(PLANE_CHUNKS[:c]) for c in range(len(PLANE_CHUNKS))]
+
+        def load_planes(c):
+            cols = slice(plane_starts[c], plane_starts[c] + PLANE_CHUNKS[c])
+            for quad in range(4):
+                nc.sync.dma_start(
+                    w4_planes[c][32 * quad : 32 * quad + 4].bitcast(I32),
+                    w4_scale_rows[4 * quad : 4 * quad + 4, :, cols].bitcast(I32),
+                )
+
+        load_planes(0)
         nc.sync.dma_start(place[:], offs2)
+        load_w8(1)
         load_w8(2)
+        load_planes(1)
         load_w8(3)
         load_w4(1)
         load_w8(4)
@@ -140,6 +152,10 @@ def tile_list_tabhs_o_silu_kernel(tc, tab, w8, w4_words, w4_scales, b, wgo, offs
         nc.scalar.copy(out=bias[:], in_=b_turned[:, 0:ROW_TILES])
 
         quantise_w8(1)
+        for tag in ("words1", "staged1"):
+            page = held.tile([P, T], F32, name=f"page{len(pages)}", tag=tag, align_bytes=64)
+            nc.gpsimd.memset(page[:], 0.0)
+            pages.append(page)
 
         for i in range(ROW_TILES):
             n0 = i * P
@@ -148,6 +164,7 @@ def tile_list_tabhs_o_silu_kernel(tc, tab, w8, w4_words, w4_scales, b, wgo, offs
             if last_of_chunk and 0 < c8 < len(W8_CHUNKS) - 1:
                 quantise_w8(c8 + 1)
             c4, o4 = chunk_of(w4_starts, n0)
+            cp, op = chunk_of(plane_starts, n0)
             page = pages[i % PAGES]
 
             def pass_e4m3(y, cols, **flags):
@@ -164,7 +181,7 @@ def tile_list_tabhs_o_silu_kernel(tc, tab, w8, w4_words, w4_scales, b, wgo, offs
                 nc.tensor.matmul_mx(
                     out=y,
                     lhsT=w4_codes[c4][:, a - 1, 2 * o4 : 2 * (o4 + P)].bitcast(FP4X4),
-                    lhsT_scale=w4_planes[:, a - 1, n0 : n0 + P],
+                    lhsT_scale=w4_planes[cp][:, a - 1, op : op + P],
                     rhs=v_codes[a][:, cols].bitcast(FP8X4),
                     rhs_scale=v_scales[a][:, cols],
                     **flags,

@@ -24,8 +24,8 @@ ROW_TILES = M // P
 HALF = S // 2
 WORD_BYTES = P * PACK * T
 W8_CHUNKS = (128, 128, 128, 128, 256, 256)
-W4_CHUNKS = (256, 256, 512)
-PLANE_CHUNKS = (256, 768)
+W4_CHUNKS = (512, 512)
+PLANE_CHUNKS = (512, 512)
 PAGES = 4
 
 
@@ -40,9 +40,9 @@ def tile_list_tabhs_o_silu_kernel(tc, tab, w8, w4_words, w4_scales, b, wgo, offs
         tab_scales = held.tile([P, PASSES, T], U8, name="tab_scales", tag="scale_window", align_bytes=64)
         w4_planes = [held.tile([P, PASSES - 1, w], U8, name=f"w4_planes{c}", align_bytes=64) for c, w in enumerate(PLANE_CHUNKS)]
         b_rows = held.tile([P, P], F32, name="b_rows")
+        identity = held.tile([P, P], F32, name="identity")
         warm_in = held.tile([P, 1], F32, name="warm_in")
         warm_out = held.tile([P, 1], F32, name="warm_out")
-        identity = held.tile([P, P], F32, name="identity")
         pages = [held.tile([P, T], F32, name=f"page{i}") for i in range(2)]
 
         nc.vector.memset(tab_scales[:].bitcast(I32), 0)
@@ -62,7 +62,7 @@ def tile_list_tabhs_o_silu_kernel(tc, tab, w8, w4_words, w4_scales, b, wgo, offs
 
         w8_rows = w8.rearrange("(p i) n -> p i n", i=PACK)
         w8_starts = [sum(W8_CHUNKS[:c]) for c in range(len(W8_CHUNKS))]
-        w8_raw = [held.tile([P, PACK, w], F32, name=f"w8_raw{c}", tag=f"raw{c}") for c, w in enumerate(W8_CHUNKS)]
+        w8_raw = [held.tile([P, PACK, w], F32, name=f"w8_raw{c}", tag=f"raw{c}", align_bytes=64) for c, w in enumerate(W8_CHUNKS)]
         w4_rows = w4_words.rearrange("a p x -> p a x")
         w4_starts = [sum(W4_CHUNKS[:c]) for c in range(len(W4_CHUNKS))]
         w4_codes = [held.tile([P, PASSES - 1, 2 * w], U8, name=f"w4_codes{c}", align_bytes=64) for c, w in enumerate(W4_CHUNKS)]
@@ -99,11 +99,10 @@ def tile_list_tabhs_o_silu_kernel(tc, tab, w8, w4_words, w4_scales, b, wgo, offs
         nc.sync.dma_start(place[:], offs2)
         load_w8(1)
         load_w8(2)
-        load_planes(1)
         load_w8(3)
         load_w4(1)
+        load_planes(1)
         load_w8(4)
-        load_w4(2)
         load_w8(5)
 
         w8_codes = [held.tile([P, w], U32, name=f"w8_codes{c}", align_bytes=64) for c, w in enumerate(W8_CHUNKS)]
@@ -146,64 +145,63 @@ def tile_list_tabhs_o_silu_kernel(tc, tab, w8, w4_words, w4_scales, b, wgo, offs
                 window = tab_words[1][:, a - 1, :].bitcast(U32)
                 nc.vector.tensor_copy(v_codes[a][:, halves[h]], window.indirect(pick[:, list_halves[h]]))
 
-        b_turned = psum.tile([P, P], F32, name="b_turned", tag=f"bank{ROW_TILES - 1}")
+        b_turned = psum.tile([P, P], F32, name="b_turned", tag="bank_b")
         nc.tensor.transpose(b_turned[:], b_rows[:], identity[:])
-        bias = held.tile([P, ROW_TILES], F32, name="bias")
-        nc.scalar.copy(out=bias[:], in_=b_turned[:, 0:ROW_TILES])
 
-        quantise_w8(1)
-        for tag in ("words1", "staged1"):
+        items = [(0, halves[h], list_halves[h]) for h in range(2)]
+        items.extend((i, slice(0, S), slice(0, S // 16)) for i in range(1, ROW_TILES))
+        follows = {w8_starts[c] // P - 1: c for c in range(1, len(W8_CHUNKS))}
+
+        biases = []
+        for u, (i, cols, entries) in enumerate(items):
+            tag = f"staged{follows[u]}" if u in follows else ("raw0" if u == len(items) - 1 else f"bias{u}")
+            biases.append(held.tile([P, 1], F32, name=f"bias{u}", tag=tag, align_bytes=64))
+        for u in reversed(range(len(items))):
+            i = items[u][0]
+            nc.scalar.copy(out=biases[u][:], in_=b_turned[:, i : i + 1])
+
+        def clear_page(tag):
             page = held.tile([P, T], F32, name=f"page{len(pages)}", tag=tag, align_bytes=64)
             nc.gpsimd.memset(page[:], 0.0)
             pages.append(page)
 
-        for i in range(ROW_TILES):
+        clear_page("words1")
+        for u, (i, cols, entries) in enumerate(items):
             n0 = i * P
             c8, o8 = chunk_of(w8_starts, n0)
-            last_of_chunk = o8 + P == W8_CHUNKS[c8]
-            if last_of_chunk and 0 < c8 < len(W8_CHUNKS) - 1:
-                quantise_w8(c8 + 1)
             c4, o4 = chunk_of(w4_starts, n0)
-            cp, op = chunk_of(plane_starts, n0)
+            width = cols.stop - cols.start
+            y = psum.tile([P, width], F32, name=f"y{u}", tag=f"bank{u % 3}")
+            steps = [(a, h) for a in range(1, PASSES) for h in range(cols.start // HALF, cols.stop // HALF)]
+            steps = [(0, None)] + steps if i == 0 else steps + [(0, None)]
+            for j, (a, h) in enumerate(steps):
+                flags = dict(start=(j == 0), stop=(j == len(steps) - 1))
+                if a == 0:
+                    nc.tensor.matmul_mx(
+                        out=y[:],
+                        lhsT=w8_codes[c8][:, o8 : o8 + P].bitcast(FP8X4),
+                        lhsT_scale=w8_planes[c8][:, o8 : o8 + P],
+                        rhs=v_codes[0][:, cols].bitcast(FP8X4),
+                        rhs_scale=v_scales[0][:, cols],
+                        **flags,
+                    )
+                else:
+                    nc.tensor.matmul_mx(
+                        out=y[:, h * HALF - cols.start : (h + 1) * HALF - cols.start],
+                        lhsT=w4_codes[c4][:, a - 1, 2 * o4 : 2 * (o4 + P)].bitcast(FP4X4),
+                        lhsT_scale=w4_planes[c4][:, a - 1, o4 : o4 + P],
+                        rhs=v_codes[a][:, halves[h]].bitcast(FP8X4),
+                        rhs_scale=v_scales[a][:, halves[h]],
+                        **flags,
+                    )
+            act_tag = f"raw{follows[u - 1]}" if u - 1 in follows else f"act{u}"
+            act = held.tile([P, width], F32, name=f"act{u}", tag=act_tag, align_bytes=64)
+            nc.scalar.activation(out=act[:], in_=y[:], func=SILU, bias=biases[u][:])
             page = pages[i % PAGES]
-
-            def pass_e4m3(y, cols, **flags):
-                nc.tensor.matmul_mx(
-                    out=y,
-                    lhsT=w8_codes[c8][:, o8 : o8 + P].bitcast(FP8X4),
-                    lhsT_scale=w8_planes[c8][:, o8 : o8 + P],
-                    rhs=v_codes[0][:, cols].bitcast(FP8X4),
-                    rhs_scale=v_scales[0][:, cols],
-                    **flags,
-                )
-
-            def pass_e2m1(y, a, cols, **flags):
-                nc.tensor.matmul_mx(
-                    out=y,
-                    lhsT=w4_codes[c4][:, a - 1, 2 * o4 : 2 * (o4 + P)].bitcast(FP4X4),
-                    lhsT_scale=w4_planes[cp][:, a - 1, op : op + P],
-                    rhs=v_codes[a][:, cols].bitcast(FP8X4),
-                    rhs_scale=v_scales[a][:, cols],
-                    **flags,
-                )
-
-            tag = f"raw{c8 + 1}" if last_of_chunk else f"act{i}"
-            if i == 0:
-                for h in range(2):
-                    y = psum.tile([P, HALF], F32, name=f"y0{h}", tag=("bank0", f"bank{ROW_TILES - 2}")[h])
-                    pass_e4m3(y[:], halves[h], start=True, stop=False)
-                    for a in range(1, PASSES):
-                        pass_e2m1(y[:], a, halves[h], start=False, stop=(a == PASSES - 1))
-                    act = held.tile([P, HALF], F32, name=f"act0{h}", tag=("act0", tag)[h])
-                    nc.scalar.activation(out=act[:], in_=y[:], func=SILU, bias=bias[:, i : i + 1])
-                    nc.vector.tensor_tensor(page[:].indirect(place[:, list_halves[h]]), act[:], gain[:, halves[h]], MULT)
-            else:
-                y = psum.tile([P, S], F32, name=f"y{i}", tag=f"bank{i}")
-                for a in range(1, PASSES):
-                    for h in range(2):
-                        pass_e2m1(y[:, halves[h]], a, halves[h], start=(a == 1 and h == 0), stop=False)
-                pass_e4m3(y[:], slice(0, S), start=False, stop=True)
-                act = held.tile([P, S], F32, name=f"act{i}", tag=tag)
-                nc.scalar.activation(out=act[:], in_=y[:], func=SILU, bias=bias[:, i : i + 1])
-                nc.vector.tensor_tensor(page[:].indirect(place[:]), act[:], gain[:], MULT)
-            nc.sync.dma_start(out[n0 : n0 + P, :], page[:])
+            nc.vector.tensor_tensor(page[:].indirect(place[:, entries]), act[:], gain[:, cols], MULT)
+            if cols.stop == S:
+                nc.sync.dma_start(out[n0 : n0 + P, :], page[:])
+            if u in follows:
+                quantise_w8(follows[u])
+            if u == 0:
+                clear_page("staged1")

from contextlib import ExitStack

import concourse.mybir as mybir
from concourse.masks import make_identity

K, M, T, S = 2048, 1024, 512, 256
FLOPS = 2 * K * M * S

F32 = mybir.dt.float32
BF16 = mybir.dt.bfloat16
I32 = mybir.dt.int32
U32 = mybir.dt.uint32
U16 = mybir.dt.uint16
U8 = mybir.dt.uint8
FP8X4 = mybir.dt.float8_e4m3fn_x4
FP4X4 = mybir.dt.float4_e2m1fn_x4
SILU = mybir.ActivationFunctionType.Silu
MULT = mybir.AluOpType.mult

P = 128
PACK = 4
PASSES = K // (P * PACK)
ROW_TILES = M // P
HALF = S // 2
WORD_BYTES = P * PACK * T
W8_CHUNKS = (128, 128, 128, 128, 256, 256)
W4_CHUNKS = (512, 512)
PLANE_CHUNKS = (512, 512)
PAGES = 4


def tile_list_tabhs_o_silu_kernel(tc, tab, w8, w4_words, w4_scales, b, wgo, offs, offs2, out):
    nc = tc.nc
    with ExitStack() as ctx:
        held = ctx.enter_context(tc.tile_pool(name="held", bufs=1))
        psum = ctx.enter_context(tc.psum_pool(name="psum", bufs=1))

        pick = held.tile([P, S // 16], U16, name="pick")
        place = held.tile([P, S // 16], U16, name="place")
        tab_scales = held.tile([P, PASSES, T], U8, name="tab_scales", tag="scale_window", align_bytes=64)
        w4_planes = [held.tile([P, PASSES - 1, w], U8, name=f"w4_planes{c}", align_bytes=64) for c, w in enumerate(PLANE_CHUNKS)]
        b_rows = held.tile([P, P], F32, name="b_rows")
        identity = held.tile([P, P], F32, name="identity")
        warm_in = held.tile([P, 1], F32, name="warm_in")
        warm_out = held.tile([P, 1], F32, name="warm_out")
        pages = [held.tile([P, T], F32, name=f"page{i}") for i in range(2)]

        nc.vector.memset(tab_scales[:].bitcast(I32), 0)
        nc.vector.memset(warm_in[:], 0.0)
        for planes in w4_planes:
            nc.vector.memset(planes[:].bitcast(I32), 0)
        nc.gpsimd.memset(b_rows[:], 0.0)
        nc.gpsimd.dma_start(b_rows[0:ROW_TILES, :], b.rearrange("(i p) -> i p", p=P))
        make_identity(nc, identity[:])
        gain = held.tile([P, S], F32, name="gain")
        nc.gpsimd.dma_start(gain[:], wgo)
        for page in pages:
            nc.vector.memset(page[:], 0.0)

        nc.sync.dma_start(pick[:], offs)
        nc.scalar.activation(out=warm_out[:], in_=warm_in[:], func=SILU)

        w8_rows = w8.rearrange("(p i) n -> p i n", i=PACK)
        w8_starts = [sum(W8_CHUNKS[:c]) for c in range(len(W8_CHUNKS))]
        w8_raw = [held.tile([P, PACK, w], F32, name=f"w8_raw{c}", tag=f"raw{c}", align_bytes=64) for c, w in enumerate(W8_CHUNKS)]
        w4_rows = w4_words.rearrange("a p x -> p a x")
        w4_starts = [sum(W4_CHUNKS[:c]) for c in range(len(W4_CHUNKS))]
        w4_codes = [held.tile([P, PASSES - 1, 2 * w], U8, name=f"w4_codes{c}", align_bytes=64) for c, w in enumerate(W4_CHUNKS)]

        def load_w8(c):
            nc.sync.dma_start(w8_raw[c][:], w8_rows[:, :, w8_starts[c] : w8_starts[c] + W8_CHUNKS[c]])

        def load_w4(c):
            cols = slice(2 * w4_starts[c], 2 * (w4_starts[c] + W4_CHUNKS[c]))
            nc.sync.dma_start(w4_codes[c][:].bitcast(I32), w4_rows[:, :, cols].bitcast(I32))

        tab_word_rows = tab[:, :WORD_BYTES].rearrange("a (p x) -> p a x", p=P).bitcast(I32)
        groups = ((0, 1), (1, PASSES))
        tab_words = [held.tile([P, a1 - a0, T], I32, name=f"tab_words{a0}", tag=f"words{a0}", align_bytes=64) for a0, a1 in groups]
        nc.sync.dma_start(tab_words[0][:], tab_word_rows[:, 0:1, :])
        tab_scale_rows = tab[:, WORD_BYTES:].rearrange("a (q t) -> q a t", t=T).bitcast(I32)
        for quad in range(4):
            nc.sync.dma_start(tab_scales[32 * quad : 32 * quad + 4].bitcast(I32), tab_scale_rows[4 * quad : 4 * quad + 4])
        load_w8(0)
        nc.sync.dma_start(tab_words[1][:], tab_word_rows[:, 1:PASSES, :])
        load_w4(0)
        w4_scale_rows = w4_scales.rearrange("a q n -> q a n")
        plane_starts = [sum(PLANE_CHUNKS[:c]) for c in range(len(PLANE_CHUNKS))]

        def load_planes(c):
            cols = slice(plane_starts[c], plane_starts[c] + PLANE_CHUNKS[c])
            for quad in range(4):
                nc.sync.dma_start(
                    w4_planes[c][32 * quad : 32 * quad + 4].bitcast(I32),
                    w4_scale_rows[4 * quad : 4 * quad + 4, :, cols].bitcast(I32),
                )

        load_planes(0)
        nc.sync.dma_start(place[:], offs2)
        load_w8(1)
        load_w8(2)
        load_w8(3)
        load_w4(1)
        load_planes(1)
        load_w8(4)
        load_w8(5)

        w8_codes = [held.tile([P, w], U32, name=f"w8_codes{c}", align_bytes=64) for c, w in enumerate(W8_CHUNKS)]
        w8_planes = [held.tile([P, w], U8, name=f"w8_planes{c}", align_bytes=64) for c, w in enumerate(W8_CHUNKS)]

        def chunk_of(starts, n0):
            c = max(j for j, s in enumerate(starts) if s <= n0)
            return c, n0 - starts[c]

        def quantise_w8(c):
            grouped = held.tile([P, W8_CHUNKS[c], PACK], BF16, name=f"w8_grouped{c}", tag=f"staged{c}", align_bytes=64)
            for o in range(0, W8_CHUNKS[c], P):
                nc.scalar.copy(
                    out=grouped[:, o : o + P, :].rearrange("p (c j) i -> p c i j", j=4),
                    in_=w8_raw[c][:, :, o : o + P].rearrange("p i (c j) -> p c i j", j=4),
                )
            nc.vector.quantize_mx(
                out=w8_codes[c][:].bitcast(FP8X4),
                scales=w8_planes[c][:],
                in_=grouped[:].rearrange("p n i -> p (n i)"),
            )

        v_codes, v_scales = [], []

        halves = [slice(h * HALF, (h + 1) * HALF) for h in range(2)]
        list_halves = [slice(h * HALF // 16, (h + 1) * HALF // 16) for h in range(2)]
        v_codes.append(held.tile([P, S], U32, name="v_codes0", align_bytes=64)[:])
        nc.vector.tensor_copy(v_codes[0], tab_words[0][:, 0, :].bitcast(U32).indirect(pick[:]))
        for a in range(PASSES):
            if a == PASSES - 1:
                quantise_w8(0)
            tag = "staged0" if a == PASSES - 1 else f"v_scales{a}"
            v_scales.append(held.tile([P, S], U8, name=f"v_scales{a}", tag=tag, align_bytes=64))
            nc.vector.tensor_copy(v_scales[a][:], tab_scales[:, a, :].indirect(pick[:]))
        later = held.tile([P, (PASSES - 1) * S], U32, name="v_codes_later", tag="scale_window", align_bytes=64)
        for a in range(1, PASSES):
            v_codes.append(later[:, (a - 1) * S : a * S])
        for h in range(2):
            for a in range(1, PASSES):
                window = tab_words[1][:, a - 1, :].bitcast(U32)
                nc.vector.tensor_copy(v_codes[a][:, halves[h]], window.indirect(pick[:, list_halves[h]]))

        b_turned = psum.tile([P, P], F32, name="b_turned", tag="bank_b")
        nc.tensor.transpose(b_turned[:], b_rows[:], identity[:])

        items = [(0, halves[h], list_halves[h]) for h in range(2)]
        items.extend((i, slice(0, S), slice(0, S // 16)) for i in range(1, ROW_TILES))
        follows = {w8_starts[c] // P - 1: c for c in range(1, len(W8_CHUNKS))}

        biases = []
        for u, (i, cols, entries) in enumerate(items):
            tag = f"staged{follows[u]}" if u in follows else ("raw0" if u == len(items) - 1 else f"bias{u}")
            biases.append(held.tile([P, 1], F32, name=f"bias{u}", tag=tag, align_bytes=64))
        for u in reversed(range(len(items))):
            i = items[u][0]
            nc.scalar.copy(out=biases[u][:], in_=b_turned[:, i : i + 1])

        def clear_page(tag):
            page = held.tile([P, T], F32, name=f"page{len(pages)}", tag=tag, align_bytes=64)
            nc.gpsimd.memset(page[:], 0.0)
            pages.append(page)

        clear_page("words1")
        for u, (i, cols, entries) in enumerate(items):
            n0 = i * P
            c8, o8 = chunk_of(w8_starts, n0)
            c4, o4 = chunk_of(w4_starts, n0)
            width = cols.stop - cols.start
            y = psum.tile([P, width], F32, name=f"y{u}", tag=f"bank{u % 3}")
            steps = [(a, h) for a in range(1, PASSES) for h in range(cols.start // HALF, cols.stop // HALF)]
            steps = [(0, None)] + steps if i == 0 else steps + [(0, None)]
            for j, (a, h) in enumerate(steps):
                flags = dict(start=(j == 0), stop=(j == len(steps) - 1))
                if a == 0:
                    nc.tensor.matmul_mx(
                        out=y[:],
                        lhsT=w8_codes[c8][:, o8 : o8 + P].bitcast(FP8X4),
                        lhsT_scale=w8_planes[c8][:, o8 : o8 + P],
                        rhs=v_codes[0][:, cols].bitcast(FP8X4),
                        rhs_scale=v_scales[0][:, cols],
                        **flags,
                    )
                else:
                    nc.tensor.matmul_mx(
                        out=y[:, h * HALF - cols.start : (h + 1) * HALF - cols.start],
                        lhsT=w4_codes[c4][:, a - 1, 2 * o4 : 2 * (o4 + P)].bitcast(FP4X4),
                        lhsT_scale=w4_planes[c4][:, a - 1, o4 : o4 + P],
                        rhs=v_codes[a][:, halves[h]].bitcast(FP8X4),
                        rhs_scale=v_scales[a][:, halves[h]],
                        **flags,
                    )
            act_tag = f"raw{follows[u - 1]}" if u - 1 in follows else f"act{u}"
            act = held.tile([P, width], F32, name=f"act{u}", tag=act_tag, align_bytes=64)
            nc.scalar.activation(out=act[:], in_=y[:], func=SILU, bias=biases[u][:])
            page = pages[i % PAGES]
            nc.vector.tensor_tensor(page[:].indirect(place[:, entries]), act[:], gain[:, cols], MULT)
            if cols.stop == S:
                nc.sync.dma_start(out[n0 : n0 + P, :], page[:])
            if u in follows:
                quantise_w8(follows[u])
            if u == 0:
                clear_page("staged1")
